import numpy as np
import ml_dtypes


def mxq(x, axis, fmt="e4m3"):
    dtype, down = {"e4m3": (ml_dtypes.float8_e4m3fn, 7), "e5m2": (ml_dtypes.float8_e5m2, 14)}[fmt]
    v = np.moveaxis(np.asarray(x, np.float32).astype(ml_dtypes.bfloat16).astype(np.float64), axis, -1)
    blocks = v.reshape(v.shape[:-1] + (-1, 32))
    amax = np.abs(blocks).max(-1, keepdims=True)
    byte = np.maximum(np.where(amax > 0, np.frexp(amax)[1] - 1 + 127, 0) - down, 1)
    scale = np.exp2(byte - 127.0)
    codes = (blocks / scale).astype(np.float32).astype(dtype).astype(np.float64)
    return np.moveaxis((codes * scale).reshape(v.shape), -1, axis)


WIDE = False


def mx_kscale(k):
    if not WIDE:
        return np.ones(k)
    levels = np.array([30, -30])
    if k % 512:
        return np.exp2(np.random.permutation(np.resize(levels, k // 32))).repeat(32)
    a = np.empty((k // 512, 16))
    for p in range(k // 512):
        a[p, :8] = np.random.permutation(np.resize(levels, 8))
        for g in range(8):
            far = levels[np.abs(levels - a[p, g]) >= 10]
            a[p, g + 8] = far[np.random.randint(len(far))]
    return np.exp2(a.ravel()).repeat(32)


BF16 = ml_dtypes.bfloat16


def bf(x):
    return np.asarray(x, np.float32).astype(BF16)


def f64(x):
    return np.asarray(x).astype(np.float64)


E2M1 = np.array([0.0, 0.5, 1.0, 1.5, 2.0, 3.0, 4.0, 6.0, -0.0, -0.5, -1.0, -1.5, -2.0, -3.0, -4.0, -6.0])


def pack_weight(w, fmt):
    k, n = w.shape
    w = f64(bf(w)).reshape(k // 32, 32, n)
    amax = np.abs(w).max(1)
    if fmt == "e4m3":
        byte = np.frexp(amax)[1] - 1 + 127 - 7
    else:
        mant, ex = np.frexp(amax / 6.0)
        byte = np.where(mant > 0.5, ex, ex - 1) + 127
    byte = np.clip(np.where(amax > 0, byte, 1), 1, 254)
    scaled = (w * np.exp2(127.0 - byte)[:, None, :]).reshape(k, n).astype(np.float32)
    by_word = np.ascontiguousarray(scaled.reshape(k // 512, 128, 4, n).transpose(0, 1, 3, 2))
    if fmt == "e4m3":
        words = by_word.astype(ml_dtypes.float8_e4m3fn).view(np.uint8)
    else:
        c = by_word.astype(ml_dtypes.float4_e2m1fn).view(np.uint8) & 0xF
        words = c[..., 0::2] | (c[..., 1::2] << 4)
    return np.ascontiguousarray(words), np.ascontiguousarray(byte.astype(np.uint8).reshape(k // 512, 16, n))


def unpack_weight(words, scales, fmt):
    g, p, n, _ = words.shape
    if fmt == "e4m3":
        vals = np.ascontiguousarray(words).view(ml_dtypes.float8_e4m3fn).astype(np.float64)
    else:
        nib = np.empty((g, p, n, 4), np.uint8)
        nib[..., 0::2] = words & 0xF
        nib[..., 1::2] = words >> 4
        vals = E2M1[nib]
    vals = vals * np.repeat(np.exp2(scales.astype(np.float64) - 127.0), 8, axis=1)[..., None]
    return vals.transpose(0, 1, 3, 2).reshape(g * 512, n)
def pack4(w):
    words, scales = pack_weight(w, "e2m1")
    return words.reshape(words.shape[0], 128, -1), scales


def unpack4(words, scales):
    return unpack_weight(words.reshape(words.shape[0], 128, -1, 2), scales, "e2m1")


M, K, F, N = 1024, 1024, 2048, 512


def setup_inputs():
    s, t = mx_kscale(K), mx_kscale(F)
    angle = np.random.uniform(-np.pi, np.pi, K)
    w = np.random.standard_normal((K, F)) / np.sqrt(K) / s[:, None]
    stiff_words, stiff_scales = pack4(w)
    return {"gamma_xz": bf(np.random.standard_normal((M, K)) * s),
            "gamma_yz": bf(np.random.standard_normal((M, K)) * s),
            "cos_ply": bf(np.cos(angle)),
            "sin_ply": bf(np.sin(angle)),
            "stiff_words": stiff_words,
            "stiff_scales": stiff_scales,
            "tau0": bf(0.4 * np.random.standard_normal(F)),
            "thick": bf(np.random.uniform(0.5, 1.5, F) * t),
            "shapes": bf(np.random.standard_normal((F, N)) / np.sqrt(F) / t[:, None])}


def reference(gamma_xz, gamma_yz, cos_ply, sin_ply, stiff_words, stiff_scales, tau0, thick, shapes):
    strain = f64(gamma_xz) * f64(cos_ply) + f64(gamma_yz) * f64(sin_ply)
    stress = mxq(strain, 1, "e4m3") @ unpack4(stiff_words, stiff_scales)
    force = (stress + f64(tau0)) * f64(thick)
    return mxq(force, 1, "e5m2") @ mxq(f64(shapes), 0, "e4m3")

@@ -1,0 +1,394 @@
+from contextlib import ExitStack
+
+import concourse.mybir as mybir
+from concourse.masks import make_identity
+
+M, K, F, N = 1024, 1024, 2048, 512
+FLOPS = 2 * M * K * F + 2 * M * F * N
+
+F32 = mybir.dt.float32
+BF16 = mybir.dt.bfloat16
+I32 = mybir.dt.int32
+U32 = mybir.dt.uint32
+U8 = mybir.dt.uint8
+E4M3 = mybir.dt.float8_e4m3fn_x4
+E5M2 = mybir.dt.float8_e5m2_x4
+E2M1 = mybir.dt.float4_e2m1fn_x4
+ALU = mybir.AluOpType
+ACT = mybir.ActivationFunctionType
+
+P = 128
+PACK = 4
+PASS = P * PACK
+HALF = 512
+HALVES = M // HALF
+K_PASSES = K // PASS
+F_PASSES = F // PASS
+RUN = 8
+
+
+def tile_laminate_shear_resultants_s9_kernel(
+    tc, gamma_xz, gamma_yz, cos_ply, sin_ply, stiff_words, stiff_scales, tau0, thick, shapes, out
+):
+    nc = tc.nc
+    with ExitStack() as ctx:
+        keep = ctx.enter_context(tc.tile_pool(name="keep", bufs=1))
+        psum = ctx.enter_context(tc.psum_pool(name="psum", bufs=1))
+        ctx.enter_context(tc.manual_schedule())
+
+        def sb(name, shape, dtype, tag=None, bufs=1):
+            return keep.tile(shape, dtype, name=name, tag=tag or name, bufs=bufs, align_bytes=64)
+
+        bank = [psum.tile([P, 512], F32, name="bank%d" % b) for b in range(8)]
+
+        ident = sb("ident", [P, P], F32)
+        ident_bf = sb("ident_bf", [P, P], BF16)
+        make_identity(nc, ident[:])
+        make_identity(nc, ident_bf[:])
+
+        vec_rows = sb("vec_rows", [P, PASS], BF16)
+        w_scale_raw = sb("w_scale_raw", [P, K_PASSES, F], U8)
+        nc.vector.memset(vec_rows[:], 0.0)
+        nc.vector.memset(w_scale_raw[:].rearrange("p g n -> p (g n)").bitcast(I32), 0)
+
+        gamma = {}
+
+        def load_gamma(x, h, kg):
+            src = (gamma_xz, gamma_yz)[x]
+            t = sb("gamma%d%d%d" % (x, h, kg), [P, 4, PASS], BF16)
+            rows = src[h * HALF : (h + 1) * HALF, kg * PASS : (kg + 1) * PASS]
+            nc.sync.dma_start(out=t[:], in_=rows.rearrange("(a p) k -> p a k", p=P))
+            gamma[x, h, kg] = t
+
+        cos_bf = sb("cos_bf", [P, K_PASSES, PACK], BF16)
+        sin_bf = sb("sin_bf", [P, K_PASSES, PACK], BF16)
+        cos_f = sb("cos_f", [P, K_PASSES, PACK], F32)
+        sin_f = sb("sin_f", [P, K_PASSES, PACK], F32)
+        warm = sb("warm", [P, 2], F32)
+
+        def load_vectors():
+            nc.scalar.dma_start(out=cos_bf[:], in_=cos_ply.rearrange("(g p t) -> p g t", p=P, t=PACK))
+            nc.scalar.dma_start(out=sin_bf[:], in_=sin_ply.rearrange("(g p t) -> p g t", p=P, t=PACK))
+            for r, vec in enumerate((tau0, thick)):
+                nc.scalar.dma_start(
+                    out=vec_rows[PACK * r : PACK * (r + 1), :].rearrange("t (b i) -> t b i", i=RUN),
+                    in_=vec.rearrange("(b t i) -> t b i", t=PACK, i=RUN),
+                )
+            nc.scalar.activation(out=warm[:, 0:1], in_=ident[:, 0:1], func=ACT.Copy)
+            nc.vector.tensor_copy(out=cos_f[:], in_=cos_bf[:])
+            nc.vector.tensor_copy(out=sin_f[:], in_=sin_bf[:])
+
+        def load_w_scales():
+            for q in range(4):
+                nc.sync.dma_start(
+                    out=w_scale_raw[32 * q : 32 * q + 4, :, :].bitcast(I32),
+                    in_=stiff_scales[:, 4 * q : 4 * q + 4, :].rearrange("g r n -> r g n").bitcast(I32),
+                )
+
+        w_raw = {}
+
+        def load_w(c):
+            t = sb("w_raw%d" % c, [P, K_PASSES, 2048], U8)
+            src = stiff_words[:, :, c * 2048 : (c + 1) * 2048].rearrange("g p n -> p g n")
+            nc.sync.dma_start(out=t[:].bitcast(I32), in_=src.bitcast(I32))
+            w_raw[c] = t
+
+        shapes_raw = {}
+
+        def load_shapes(g):
+            t = sb("shapes_raw%d" % g, [P, PACK, N], BF16)
+            src = shapes[g * PASS : (g + 1) * PASS, :].rearrange("(j t i) n -> t j i n", t=PACK, i=RUN)
+            for s in range(PACK):
+                nc.sync.dma_start(out=t[:, s, :], in_=src[s])
+            shapes_raw[g] = t
+
+        def turn(x, h, kg, banks):
+            words = gamma[x, h, kg][:].bitcast(F32)
+            for u in range(2):
+                for a in range(4):
+                    nc.tensor.transpose(bank[banks[u]][:, a * P : (a + 1) * P], words[:, a, u::2], ident[:])
+
+        def turned(b, e):
+            return bank[b][:].bitcast(BF16).rearrange("p (m e) -> p m e", e=2)[:, :, e]
+
+        def load_pair(x, ap):
+            src = (gamma_xz, gamma_yz)[x]
+            t = sb("gamma_first%d%d" % (x, ap), [P, 2, PASS], BF16)
+            rows = src[ap * 256 : (ap + 1) * 256, 0:PASS]
+            nc.sync.dma_start(out=t[:], in_=rows.rearrange("(a p) k -> p a k", p=P))
+            gamma[x, "pair", ap] = t
+
+        def turn_pair(x, ap, b):
+            words = gamma[x, "pair", ap][:].bitcast(F32)
+            for u in range(2):
+                for a in range(2):
+                    c0 = (2 * u + a) * P
+                    nc.tensor.transpose(bank[b][:, c0 : c0 + P], words[:, a, u::2], ident[:])
+
+        def turned_pair(b, t):
+            return bank[b][:].bitcast(BF16).rearrange("p (u m e) -> p u m e", u=2, e=2)[:, t // 2, :, t % 2]
+
+        def strain_a_pair(ap, b):
+            for t in range(PACK):
+                d = sb("prod_first%d%d" % (ap, t), [P, 256], F32)
+                nc.scalar.activation(out=d[:], in_=turned_pair(b, t), func=ACT.Copy, scale=cos_f[:, 0, t : t + 1])
+                prod["pair", ap, t] = d
+
+        def strain_b_pair(ap, b):
+            if (0, 0) not in s_rows:
+                s_rows[0, 0] = sb("s_rows00", [P, PACK, HALF], BF16)
+            for t in range(PACK):
+                nc.vector.scalar_tensor_tensor(
+                    out=s_rows[0, 0][:, t, ap * 256 : (ap + 1) * 256], in0=turned_pair(b, t), scalar=sin_f[:, 0, t : t + 1],
+                    in1=prod["pair", ap, t][:], op0=ALU.mult, op1=ALU.add,
+                )
+
+        prod = {}
+
+        def strain_a(h, kg, banks, ts=range(PACK)):
+            for t in ts:
+                d = sb("prod%d%d%d" % (h, kg, t), [P, HALF], F32, tag="prod", bufs=8)
+                nc.scalar.activation(out=d[:], in_=turned(banks[t // 2], t % 2), func=ACT.Copy, scale=cos_f[:, kg, t : t + 1])
+                prod[h, kg, t] = d
+
+        s_rows = {}
+
+        def strain_b(h, kg, banks, ts):
+            if (h, kg) not in s_rows:
+                s_rows[h, kg] = sb("s_rows%d%d" % (h, kg), [P, PACK, HALF], BF16)
+            for t in ts:
+                nc.vector.scalar_tensor_tensor(
+                    out=s_rows[h, kg][:, t, :], in0=turned(banks[t // 2], t % 2), scalar=sin_f[:, kg, t : t + 1],
+                    in1=prod[h, kg, t][:], op0=ALU.mult, op1=ALU.add,
+                )
+
+        woven = {}
+
+        def weave(key, rows, eng, lo=0, hi=512):
+            if key not in woven:
+                woven[key] = sb("woven_%s" % key, [P, 512, PACK], BF16, tag="woven", bufs=5)
+            dst = woven[key][:, lo:hi, :].rearrange("p (c i) t -> p c t i", i=4)
+            src = rows[:, :, lo:hi].rearrange("p t (c i) -> p c t i", i=4)
+            if eng == "act":
+                nc.scalar.copy(out=dst, in_=src)
+            else:
+                nc.vector.tensor_copy(out=dst, in_=src)
+
+        codes = {}
+
+        def quantise(key, fmt, lo=0, hi=512):
+            if key not in codes:
+                codes[key] = (sb("codes_%s" % key, [P, 512], U32), sb("scales_%s" % key, [P, 512], U8))
+            c, s = codes[key]
+            nc.vector.quantize_mx(
+                out=c[:, lo:hi].bitcast(fmt), scales=s[:, lo:hi], in_=woven[key][:, lo:hi, :].rearrange("p n t -> p (n t)")
+            )
+
+        tau_thick = sb("tau_thick", [P, F_PASSES, 2 * PACK], F32)
+        bias = sb("bias", [P, F_PASSES, PACK], F32)
+
+        def turn_vectors(b):
+            view = bank[b][:].bitcast(BF16)[:, 0:PASS].rearrange("p (g r) -> p g r", r=P)
+            for g in range(F_PASSES):
+                nc.tensor.transpose(view[:, g, :], vec_rows[:, g * P : (g + 1) * P], ident_bf[:])
+
+        def copy_vectors(b):
+            view = bank[b][:].bitcast(BF16)[:, 0:PASS].rearrange("p (g r) -> p g r", r=P)
+            nc.scalar.copy(out=tau_thick[:], in_=view[:, :, 0 : 2 * PACK])
+
+        def make_bias():
+            nc.vector.tensor_tensor(out=bias[:], in0=tau_thick[:, :, 0:PACK], in1=tau_thick[:, :, PACK : 2 * PACK], op=ALU.mult)
+
+        w_codes = {}
+        w_scale = sb("w_scale", [P, PACK, K_PASSES * F_PASSES * P], U8)
+
+        def order_w(c):
+            d = sb("w_codes%d" % c, [P, PACK, 1024], U8)
+            nc.vector.tensor_copy(
+                out=d[:].bitcast(I32).rearrange("p t (b w) -> p b t w", w=4),
+                in_=w_raw[c][:].rearrange("p g n -> p (g n)").bitcast(I32).rearrange("p (b t w) -> p b t w", t=PACK, w=4),
+            )
+            w_codes[c] = d
+
+        def order_w_scales():
+            nc.vector.tensor_copy(
+                out=w_scale[:].bitcast(I32).rearrange("p t (b w) -> p t b w", w=2),
+                in_=w_scale_raw[:].rearrange("p g n -> p (g n)").bitcast(I32).rearrange("p (b t w) -> p t b w", t=PACK, w=2),
+            )
+
+        def stress(h, g, t, b):
+            for kg in range(K_PASSES):
+                col = (2 * kg + g % 2) * 256
+                scol = (F_PASSES * kg + g) * P
+                c, s = codes["s%d%d" % (h, kg)]
+                nc.tensor.matmul_mx(
+                    out=bank[b][:], lhsT=w_codes[g // 2][:, t, col : col + 256].bitcast(E2M1),
+                    lhsT_scale=w_scale[:, t, scol : scol + P], rhs=c[:].bitcast(E4M3), rhs_scale=s[:],
+                    start=(kg == 0), stop=(kg == K_PASSES - 1),
+                )
+
+        f_rows = {}
+
+        def force(h, g, t, b, eng):
+            if (h, g) not in f_rows:
+                f_rows[h, g] = sb("f_rows%d%d" % (h, g), [P, PACK, HALF], BF16, tag="f_rows", bufs=8)
+            if eng == "act":
+                nc.scalar.activation(
+                    out=f_rows[h, g][:, t, :], in_=bank[b][:], func=ACT.Identity,
+                    scale=tau_thick[:, g, PACK + t : PACK + t + 1], bias=bias[:, g, t : t + 1],
+                )
+            else:
+                nc.vector.tensor_scalar(
+                    out=f_rows[h, g][:, t, :], in0=bank[b][:], scalar1=tau_thick[:, g, t : t + 1],
+                    scalar2=tau_thick[:, g, PACK + t : PACK + t + 1], op0=ALU.add, op1=ALU.mult,
+                )
+
+        def resultants(h, g, a, b, start, stop):
+            c, s = codes["f%d%d" % (h, g)]
+            wc, ws = codes["w%d" % g]
+            nc.tensor.matmul_mx(
+                out=bank[b][:], lhsT=c[:, a * P : (a + 1) * P].bitcast(E5M2), lhsT_scale=s[:, a * P : (a + 1) * P],
+                rhs=wc[:].bitcast(E4M3), rhs_scale=ws[:], start=start, stop=stop,
+            )
+
+        def store(h, a, b, eng):
+            d = sb("res%d%d" % (h, a), [P, N], F32)
+            if eng == "act":
+                nc.scalar.copy(out=d[:], in_=bank[b][:])
+            else:
+                nc.vector.tensor_copy(out=d[:], in_=bank[b][:])
+            r0 = h * HALF + a * P
+            nc.sync.dma_start(out=out[r0 : r0 + P, :], in_=d[:])
+
+        def group(h, g, banks, engs="aaaa"):
+            for t in range(PACK):
+                stress(h, g, t, banks[t])
+                force(h, g, t, banks[t], "act" if engs[t] == "a" else "dve")
+
+        def wf(h, g, eng="dve", lo=0, hi=512):
+            weave("f%d%d" % (h, g), f_rows[h, g], eng, lo, hi)
+
+        def qf(h, g, lo=0, hi=512):
+            quantise("f%d%d" % (h, g), E5M2, lo, hi)
+
+        def ws(h, kg, eng="dve", lo=0, hi=512):
+            weave("s%d%d" % (h, kg), s_rows[h, kg], eng, lo, hi)
+
+        def qs(h, kg):
+            quantise("s%d%d" % (h, kg), E4M3)
+
+        def ww(g, eng="dve"):
+            weave("w%d" % g, shapes_raw[g], eng)
+
+        def qw(g):
+            quantise("w%d" % g, E4M3)
+
+        def res4(h, g, banks, tiles=range(4), first=0, last=3):
+            for a in tiles:
+                resultants(h, g, a, banks[a], g == first, g == last)
+
+        load_pair(0, 0)
+        load_pair(1, 0)
+        load_vectors()
+        load_pair(0, 1)
+        load_pair(1, 1)
+        load_gamma(0, 0, 1)
+        load_gamma(1, 0, 1)
+        load_gamma(0, 1, 0)
+        load_w_scales()
+        load_w(0)
+        load_gamma(1, 1, 0)
+        load_gamma(0, 1, 1)
+        load_gamma(1, 1, 1)
+        load_w(1)
+        for g in range(F_PASSES):
+            load_shapes(g)
+
+        turn_pair(0, 0, 0)
+        turn_pair(1, 0, 1)
+        strain_a_pair(0, 0)
+        turn_pair(0, 1, 2)
+        turn_pair(1, 1, 3)
+        strain_b_pair(0, 1)
+        strain_a_pair(1, 2)
+        strain_b_pair(1, 3)
+        turn_vectors(0)
+        copy_vectors(0)
+        turn(0, 0, 1, (4, 5))
+        turn(1, 0, 1, (6, 7))
+        ws(0, 0, "act", 384, 512)
+        ws(0, 0, "dve", 0, 384)
+        strain_a(0, 1, (4, 5))
+        qs(0, 0)
+        strain_b(0, 1, (6, 7), range(4))
+        turn(0, 1, 0, (1, 2))
+        strain_a(1, 0, (1, 2), (0, 1))
+        order_w_scales()
+        ws(0, 1, "act", 256, 512)
+        ws(0, 1, "dve", 0, 256)
+        order_w(0)
+        qs(0, 1)
+        make_bias()
+        strain_a(1, 0, (1, 2), (2, 3))
+        turn(1, 1, 0, (3, 0))
+        group(0, 0, (4, 5, 1, 2))
+        strain_b(1, 0, (3, 0), range(4))
+        turn(0, 1, 1, (4, 5))
+        turn(1, 1, 1, (6, 7))
+        strain_a(1, 1, (4, 5))
+        order_w(1)
+        ws(1, 0)
+        group(0, 1, (1, 2, 3, 0))
+        strain_b(1, 1, (6, 7), (0, 1))
+        qs(1, 0)
+        strain_b(1, 1, (6, 7), (2, 3))
+        group(0, 2, (4, 5, 1, 2))
+        wf(0, 0)
+        ws(1, 1)
+        qf(0, 0)
+        group(0, 3, (3, 0, 6, 7))
+        qs(1, 1)
+        RA = (4, 5, 1, 2)
+        RB = (3, 0, 6, 7)
+        for g in range(4):
+            group(1, g, (RA, RB)[g % 2])
+        ww(0)
+        wf(0, 1)
+        qw(0)
+        qf(0, 1)
+        ww(1)
+        wf(0, 2)
+        qw(1)
+        qf(0, 2)
+        ww(2)
+        res4(0, 0, RA)
+        res4(0, 1, RA)
+        ww(3)
+        qw(2)
+        res4(0, 2, RA)
+        wf(0, 3)
+        qw(3)
+        qf(0, 3)
+        res4(0, 3, RA)
+        wf(1, 3, "act", 0, 256)
+        wf(1, 2, "act", 0, 256)
+        wf(1, 3, "act", 256, 512)
+        wf(1, 0, "dve", 0, 256)
+        wf(1, 1, "dve", 0, 256)
+        for g in (0, 3, 2, 1):
+            qf(1, g, 0, 256)
+            res4(1, g, RB, (0, 1), 0, 1)
+        for a in range(4):
+            store(0, a, RA[a], "act")
+        wf(1, 0, "dve", 256, 512)
+        wf(1, 1, "dve", 256, 512)
+        for g in (3, 0, 1):
+            qf(1, g, 256, 512)
+            res4(1, g, RB, (2, 3), 3, 2)
+        wf(1, 2, "dve", 256, 512)
+        store(1, 0, RB[0], "act")
+        store(1, 1, RB[1], "act")
+        qf(1, 2, 256, 512)
+        res4(1, 2, RB, (2, 3), 3, 2)
+        store(1, 2, RB[2], "act")
+        store(1, 3, RB[3], "dve")

@@ -46,6 +46,7 @@ def tile_laminate_shear_resultants_s9_kernel(
         make_identity(nc, ident[:])
         make_identity(nc, ident_bf[:])
 
+        vec_raw = sb("vec_raw", [P, PASS], BF16)
         vec_rows = sb("vec_rows", [P, PASS], BF16)
         w_scale_raw = sb("w_scale_raw", [P, K_PASSES, F], U8)
         nc.vector.memset(vec_rows[:], 0.0)
@@ -60,23 +61,25 @@ def tile_laminate_shear_resultants_s9_kernel(
             nc.sync.dma_start(out=t[:], in_=rows.rearrange("(a p) k -> p a k", p=P))
             gamma[x, h, kg] = t
 
+        warm = sb("warm", [P, 2], F32)
+
         cos_bf = sb("cos_bf", [P, K_PASSES, PACK], BF16)
         sin_bf = sb("sin_bf", [P, K_PASSES, PACK], BF16)
         cos_f = sb("cos_f", [P, K_PASSES, PACK], F32)
         sin_f = sb("sin_f", [P, K_PASSES, PACK], F32)
-        warm = sb("warm", [P, 2], F32)
 
         def load_vectors():
             nc.scalar.dma_start(out=cos_bf[:], in_=cos_ply.rearrange("(g p t) -> p g t", p=P, t=PACK))
             nc.scalar.dma_start(out=sin_bf[:], in_=sin_ply.rearrange("(g p t) -> p g t", p=P, t=PACK))
-            for r, vec in enumerate((tau0, thick)):
-                nc.scalar.dma_start(
-                    out=vec_rows[PACK * r : PACK * (r + 1), :].rearrange("t (b i) -> t b i", i=RUN),
-                    in_=vec.rearrange("(b t i) -> t b i", t=PACK, i=RUN),
-                )
+            for r, src in enumerate((tau0, thick)):
+                nc.scalar.dma_start(out=vec_raw[4 * r : 4 * r + 4, :], in_=src.rearrange("(g c) -> g c", c=PASS))
             nc.scalar.activation(out=warm[:, 0:1], in_=ident[:, 0:1], func=ACT.Copy)
             nc.vector.tensor_copy(out=cos_f[:], in_=cos_bf[:])
             nc.vector.tensor_copy(out=sin_f[:], in_=sin_bf[:])
+            nc.vector.tensor_copy(
+                out=vec_rows[0:8, :].rearrange("r (t j i) -> r t j i", t=PACK, i=RUN),
+                in_=vec_raw[0:8, :].rearrange("r (j t i) -> r t j i", t=PACK, i=RUN),
+            )
 
         def load_w_scales():
             for q in range(4):
@@ -147,7 +150,7 @@ def tile_laminate_shear_resultants_s9_kernel(
 
         def strain_a(h, kg, banks, ts=range(PACK)):
             for t in ts:
-                d = sb("prod%d%d%d" % (h, kg, t), [P, HALF], F32, tag="prod", bufs=8)
+                d = sb("prod%d%d%d" % (h, kg, t), [P, HALF], F32, tag="prod", bufs=12)
                 nc.scalar.activation(out=d[:], in_=turned(banks[t // 2], t % 2), func=ACT.Copy, scale=cos_f[:, kg, t : t + 1])
                 prod[h, kg, t] = d
 
@@ -184,20 +187,17 @@ def tile_laminate_shear_resultants_s9_kernel(
                 out=c[:, lo:hi].bitcast(fmt), scales=s[:, lo:hi], in_=woven[key][:, lo:hi, :].rearrange("p n t -> p (n t)")
             )
 
-        tau_thick = sb("tau_thick", [P, F_PASSES, 2 * PACK], F32)
-        bias = sb("bias", [P, F_PASSES, PACK], F32)
+        vec = sb("vec", [P, PACK, 8], F32)
+        bias = sb("bias", [P, PACK, F_PASSES], F32)
 
         def turn_vectors(b):
-            view = bank[b][:].bitcast(BF16)[:, 0:PASS].rearrange("p (g r) -> p g r", r=P)
-            for g in range(F_PASSES):
-                nc.tensor.transpose(view[:, g, :], vec_rows[:, g * P : (g + 1) * P], ident_bf[:])
-
-        def copy_vectors(b):
-            view = bank[b][:].bitcast(BF16)[:, 0:PASS].rearrange("p (g r) -> p g r", r=P)
-            nc.scalar.copy(out=tau_thick[:], in_=view[:, :, 0 : 2 * PACK])
+            view = bank[b][:].bitcast(BF16)[:, 0:PASS].rearrange("p (t r) -> p t r", r=P)
+            for t in range(PACK):
+                nc.tensor.transpose(view[:, t, :], vec_rows[:, t * P : (t + 1) * P], ident_bf[:])
+            nc.scalar.copy(out=vec[:], in_=view[:, :, 0:8])
 
         def make_bias():
-            nc.vector.tensor_tensor(out=bias[:], in0=tau_thick[:, :, 0:PACK], in1=tau_thick[:, :, PACK : 2 * PACK], op=ALU.mult)
+            nc.vector.tensor_tensor(out=bias[:], in0=vec[:, :, 0:4], in1=vec[:, :, 4:8], op=ALU.mult)
 
         w_codes = {}
         w_scale = sb("w_scale", [P, PACK, K_PASSES * F_PASSES * P], U8)
@@ -235,12 +235,12 @@ def tile_laminate_shear_resultants_s9_kernel(
             if eng == "act":
                 nc.scalar.activation(
                     out=f_rows[h, g][:, t, :], in_=bank[b][:], func=ACT.Identity,
-                    scale=tau_thick[:, g, PACK + t : PACK + t + 1], bias=bias[:, g, t : t + 1],
+                    scale=vec[:, t, 4 + g : 5 + g], bias=bias[:, t, g : g + 1],
                 )
             else:
                 nc.vector.tensor_scalar(
-                    out=f_rows[h, g][:, t, :], in0=bank[b][:], scalar1=tau_thick[:, g, t : t + 1],
-                    scalar2=tau_thick[:, g, PACK + t : PACK + t + 1], op0=ALU.add, op1=ALU.mult,
+                    out=f_rows[h, g][:, t, :], in0=bank[b][:], scalar1=vec[:, t, g : g + 1],
+                    scalar2=vec[:, t, 4 + g : 5 + g], op0=ALU.add, op1=ALU.mult,
                 )
 
         def resultants(h, g, a, b, start, stop):
@@ -251,19 +251,20 @@ def tile_laminate_shear_resultants_s9_kernel(
                 rhs=wc[:].bitcast(E4M3), rhs_scale=ws[:], start=start, stop=stop,
             )
 
-        def store(h, a, b, eng):
-            d = sb("res%d%d" % (h, a), [P, N], F32)
+        def store(h, a, b, eng, lo=0, hi=N):
+            d = sb("res%d%d_%d" % (h, a, lo), [P, hi - lo], F32)
             if eng == "act":
-                nc.scalar.copy(out=d[:], in_=bank[b][:])
+                nc.scalar.copy(out=d[:], in_=bank[b][:, lo:hi])
             else:
-                nc.vector.tensor_copy(out=d[:], in_=bank[b][:])
+                nc.vector.tensor_copy(out=d[:], in_=bank[b][:, lo:hi])
             r0 = h * HALF + a * P
-            nc.sync.dma_start(out=out[r0 : r0 + P, :], in_=d[:])
+            nc.sync.dma_start(out=out[r0 : r0 + P, lo:hi], in_=d[:])
 
-        def group(h, g, banks, engs="aaaa"):
+        def group(h, g, banks, order=(0, 1, 2, 3)):
             for t in range(PACK):
                 stress(h, g, t, banks[t])
-                force(h, g, t, banks[t], "act" if engs[t] == "a" else "dve")
+            for t in order:
+                force(h, g, t, banks[t], "act")
 
         def wf(h, g, eng="dve", lo=0, hi=512):
             weave("f%d%d" % (h, g), f_rows[h, g], eng, lo, hi)
@@ -313,12 +314,12 @@ def tile_laminate_shear_resultants_s9_kernel(
         strain_a_pair(1, 2)
         strain_b_pair(1, 3)
         turn_vectors(0)
-        copy_vectors(0)
         turn(0, 0, 1, (4, 5))
         turn(1, 0, 1, (6, 7))
         ws(0, 0, "act", 384, 512)
         ws(0, 0, "dve", 0, 384)
         strain_a(0, 1, (4, 5))
+        make_bias()
         qs(0, 0)
         strain_b(0, 1, (6, 7), range(4))
         turn(0, 1, 0, (1, 2))
@@ -328,30 +329,31 @@ def tile_laminate_shear_resultants_s9_kernel(
         ws(0, 1, "dve", 0, 256)
         order_w(0)
         qs(0, 1)
-        make_bias()
         strain_a(1, 0, (1, 2), (2, 3))
         turn(1, 1, 0, (3, 0))
         group(0, 0, (4, 5, 1, 2))
-        strain_b(1, 0, (3, 0), range(4))
+        strain_b(1, 0, (3, 0), (3, 0, 1, 2))
         turn(0, 1, 1, (4, 5))
         turn(1, 1, 1, (6, 7))
         strain_a(1, 1, (4, 5))
         order_w(1)
         ws(1, 0)
-        group(0, 1, (1, 2, 3, 0))
+        group(0, 1, (1, 2, 3, 0), (1, 0, 3, 2))
         strain_b(1, 1, (6, 7), (0, 1))
         qs(1, 0)
         strain_b(1, 1, (6, 7), (2, 3))
-        group(0, 2, (4, 5, 1, 2))
+        group(0, 2, (4, 5, 2, 1), (1, 0, 3, 2))
         wf(0, 0)
         ws(1, 1)
         qf(0, 0)
-        group(0, 3, (3, 0, 6, 7))
+        group(0, 3, (0, 3, 6, 7), (1, 0, 3, 2))
         qs(1, 1)
         RA = (4, 5, 1, 2)
         RB = (3, 0, 6, 7)
-        for g in range(4):
-            group(1, g, (RA, RB)[g % 2])
+        group(1, 0, (5, 4, 1, 2), (1, 0, 3, 2))
+        group(1, 1, (3, 0, 7, 6), (1, 0, 3, 2))
+        group(1, 2, (4, 5, 2, 1), (3, 0, 1, 2))
+        group(1, 3, (6, 3, 0, 7), (1, 0, 3, 2))
         ww(0)
         wf(0, 1)
         qw(0)
@@ -390,5 +392,6 @@ def tile_laminate_shear_resultants_s9_kernel(
         store(1, 1, RB[1], "act")
         qf(1, 2, 256, 512)
         res4(1, 2, RB, (2, 3), 3, 2)
-        store(1, 2, RB[2], "act")
-        store(1, 3, RB[3], "dve")
+        for lo in (0, 256):
+            store(1, 2, RB[2], "act", lo, lo + 256)
+            store(1, 3, RB[3], "dve", lo, lo + 256)

@@ -41,6 +41,8 @@ def tile_laminate_shear_resultants_s9_kernel(
 
         bank = [psum.tile([P, 512], F32, name="bank%d" % b) for b in range(8)]
 
+        rot_rows = sb("rot_rows", [P, PASS], BF16)
+        nc.gpsimd.memset(rot_rows[:].bitcast(I32), 0)
         ident = sb("ident", [P, P], F32)
         ident_bf = sb("ident_bf", [P, P], BF16)
         make_identity(nc, ident[:])
@@ -48,9 +50,9 @@ def tile_laminate_shear_resultants_s9_kernel(
 
         vec_raw = sb("vec_raw", [P, PASS], BF16)
         vec_rows = sb("vec_rows", [P, PASS], BF16)
-        w_scale_raw = sb("w_scale_raw", [P, K_PASSES, F], U8)
+        w_scale_raw = sb("w_scale_raw", [P, 2, K_PASSES, F // 2], U8)
         nc.vector.memset(vec_rows[:], 0.0)
-        nc.vector.memset(w_scale_raw[:].rearrange("p g n -> p (g n)").bitcast(I32), 0)
+        nc.vector.memset(w_scale_raw[:].rearrange("p c g n -> p (c g n)").bitcast(I32), 0)
 
         gamma = {}
 
@@ -63,36 +65,40 @@ def tile_laminate_shear_resultants_s9_kernel(
 
         warm = sb("warm", [P, 2], F32)
 
-        cos_bf = sb("cos_bf", [P, K_PASSES, PACK], BF16)
-        sin_bf = sb("sin_bf", [P, K_PASSES, PACK], BF16)
-        cos_f = sb("cos_f", [P, K_PASSES, PACK], F32)
-        sin_f = sb("sin_f", [P, K_PASSES, PACK], F32)
+        rot = sb("rot", [P, 2, 4, 2], F32)
+
+        def turn_rot(b):
+            words = rot_rows[:].bitcast(F32)
+            for u in range(2):
+                nc.tensor.transpose(bank[b][:, u * P : (u + 1) * P], words[:, u::2], ident[:])
+            view = bank[b][:].bitcast(BF16)[:, 0:PASS].rearrange("p (u r e) -> p u r e", u=2, e=2)
+            nc.vector.tensor_copy(out=rot[:], in_=view[:, :, 0:4, :])
+
+        def load_rot():
+            for r, src in enumerate((cos_ply, sin_ply)):
+                nc.sync.dma_start(out=rot_rows[2 * r : 2 * r + 2, :], in_=src.rearrange("(g c) -> g c", c=PASS))
 
         def load_vectors():
-            nc.scalar.dma_start(out=cos_bf[:], in_=cos_ply.rearrange("(g p t) -> p g t", p=P, t=PACK))
-            nc.scalar.dma_start(out=sin_bf[:], in_=sin_ply.rearrange("(g p t) -> p g t", p=P, t=PACK))
             for r, src in enumerate((tau0, thick)):
                 nc.scalar.dma_start(out=vec_raw[4 * r : 4 * r + 4, :], in_=src.rearrange("(g c) -> g c", c=PASS))
             nc.scalar.activation(out=warm[:, 0:1], in_=ident[:, 0:1], func=ACT.Copy)
-            nc.vector.tensor_copy(out=cos_f[:], in_=cos_bf[:])
-            nc.vector.tensor_copy(out=sin_f[:], in_=sin_bf[:])
             nc.vector.tensor_copy(
                 out=vec_rows[0:8, :].rearrange("r (t j i) -> r t j i", t=PACK, i=RUN),
                 in_=vec_raw[0:8, :].rearrange("r (j t i) -> r t j i", t=PACK, i=RUN),
             )
 
-        def load_w_scales():
+        def load_w_scales(c):
             for q in range(4):
                 nc.sync.dma_start(
-                    out=w_scale_raw[32 * q : 32 * q + 4, :, :].bitcast(I32),
-                    in_=stiff_scales[:, 4 * q : 4 * q + 4, :].rearrange("g r n -> r g n").bitcast(I32),
+                    out=w_scale_raw[32 * q : 32 * q + 4, c, :, :].bitcast(I32),
+                    in_=stiff_scales[:, 4 * q : 4 * q + 4, c * 1024 : (c + 1) * 1024].rearrange("g r n -> r g n").bitcast(I32),
                 )
 
         w_raw = {}
 
         def load_w(c):
-            t = sb("w_raw%d" % c, [P, K_PASSES, 2048], U8)
-            src = stiff_words[:, :, c * 2048 : (c + 1) * 2048].rearrange("g p n -> p g n")
+            t = sb("w_raw%d" % c, [P, K_PASSES, 1024], U8)
+            src = stiff_words[:, :, c * 1024 : (c + 1) * 1024].rearrange("g p n -> p g n")
             nc.sync.dma_start(out=t[:].bitcast(I32), in_=src.bitcast(I32))
             w_raw[c] = t
 
@@ -134,7 +140,7 @@ def tile_laminate_shear_resultants_s9_kernel(
         def strain_a_pair(ap, b):
             for t in range(PACK):
                 d = sb("prod_first%d%d" % (ap, t), [P, 256], F32)
-                nc.scalar.activation(out=d[:], in_=turned_pair(b, t), func=ACT.Copy, scale=cos_f[:, 0, t : t + 1])
+                nc.scalar.activation(out=d[:], in_=turned_pair(b, t), func=ACT.Copy, scale=rot[:, t // 2, 0, t % 2 : t % 2 + 1])
                 prod["pair", ap, t] = d
 
         def strain_b_pair(ap, b):
@@ -142,7 +148,7 @@ def tile_laminate_shear_resultants_s9_kernel(
                 s_rows[0, 0] = sb("s_rows00", [P, PACK, HALF], BF16)
             for t in range(PACK):
                 nc.vector.scalar_tensor_tensor(
-                    out=s_rows[0, 0][:, t, ap * 256 : (ap + 1) * 256], in0=turned_pair(b, t), scalar=sin_f[:, 0, t : t + 1],
+                    out=s_rows[0, 0][:, t, ap * 256 : (ap + 1) * 256], in0=turned_pair(b, t), scalar=rot[:, t // 2, 2, t % 2 : t % 2 + 1],
                     in1=prod["pair", ap, t][:], op0=ALU.mult, op1=ALU.add,
                 )
 
@@ -151,7 +157,7 @@ def tile_laminate_shear_resultants_s9_kernel(
         def strain_a(h, kg, banks, ts=range(PACK)):
             for t in ts:
                 d = sb("prod%d%d%d" % (h, kg, t), [P, HALF], F32, tag="prod", bufs=12)
-                nc.scalar.activation(out=d[:], in_=turned(banks[t // 2], t % 2), func=ACT.Copy, scale=cos_f[:, kg, t : t + 1])
+                nc.scalar.activation(out=d[:], in_=turned(banks[t // 2], t % 2), func=ACT.Copy, scale=rot[:, t // 2, kg, t % 2 : t % 2 + 1])
                 prod[h, kg, t] = d
 
         s_rows = {}
@@ -161,7 +167,7 @@ def tile_laminate_shear_resultants_s9_kernel(
                 s_rows[h, kg] = sb("s_rows%d%d" % (h, kg), [P, PACK, HALF], BF16)
             for t in ts:
                 nc.vector.scalar_tensor_tensor(
-                    out=s_rows[h, kg][:, t, :], in0=turned(banks[t // 2], t % 2), scalar=sin_f[:, kg, t : t + 1],
+                    out=s_rows[h, kg][:, t, :], in0=turned(banks[t // 2], t % 2), scalar=rot[:, t // 2, 2 + kg, t % 2 : t % 2 + 1],
                     in1=prod[h, kg, t][:], op0=ALU.mult, op1=ALU.add,
                 )
 
@@ -200,30 +206,30 @@ def tile_laminate_shear_resultants_s9_kernel(
             nc.vector.tensor_tensor(out=bias[:], in0=vec[:, :, 0:4], in1=vec[:, :, 4:8], op=ALU.mult)
 
         w_codes = {}
-        w_scale = sb("w_scale", [P, PACK, K_PASSES * F_PASSES * P], U8)
+        w_scale = sb("w_scale", [P, 2, PACK, K_PASSES * 2 * P], U8)
 
         def order_w(c):
-            d = sb("w_codes%d" % c, [P, PACK, 1024], U8)
+            d = sb("w_codes%d" % c, [P, PACK, 512], U8)
             nc.vector.tensor_copy(
                 out=d[:].bitcast(I32).rearrange("p t (b w) -> p b t w", w=4),
                 in_=w_raw[c][:].rearrange("p g n -> p (g n)").bitcast(I32).rearrange("p (b t w) -> p b t w", t=PACK, w=4),
             )
             w_codes[c] = d
 
-        def order_w_scales():
+        def order_w_scales(c):
             nc.vector.tensor_copy(
-                out=w_scale[:].bitcast(I32).rearrange("p t (b w) -> p t b w", w=2),
-                in_=w_scale_raw[:].rearrange("p g n -> p (g n)").bitcast(I32).rearrange("p (b t w) -> p t b w", t=PACK, w=2),
+                out=w_scale[:, c, :, :].bitcast(I32).rearrange("p t (b w) -> p t b w", w=2),
+                in_=w_scale_raw[:, c, :, :].rearrange("p g n -> p (g n)").bitcast(I32).rearrange("p (b t w) -> p t b w", t=PACK, w=2),
             )
 
         def stress(h, g, t, b):
             for kg in range(K_PASSES):
-                col = (2 * kg + g % 2) * 256
-                scol = (F_PASSES * kg + g) * P
+                col = kg * 256
+                scol = (2 * kg + g % 2) * P
                 c, s = codes["s%d%d" % (h, kg)]
                 nc.tensor.matmul_mx(
-                    out=bank[b][:], lhsT=w_codes[g // 2][:, t, col : col + 256].bitcast(E2M1),
-                    lhsT_scale=w_scale[:, t, scol : scol + P], rhs=c[:].bitcast(E4M3), rhs_scale=s[:],
+                    out=bank[b][:], lhsT=w_codes[g][:, t, col : col + 256].bitcast(E2M1),
+                    lhsT_scale=w_scale[:, g // 2, t, scol : scol + P], rhs=c[:].bitcast(E4M3), rhs_scale=s[:],
                     start=(kg == 0), stop=(kg == K_PASSES - 1),
                 )
 
@@ -288,6 +294,7 @@ def tile_laminate_shear_resultants_s9_kernel(
             for a in tiles:
                 resultants(h, g, a, banks[a], g == first, g == last)
 
+        load_rot()
         load_pair(0, 0)
         load_pair(1, 0)
         load_vectors()
@@ -296,15 +303,19 @@ def tile_laminate_shear_resultants_s9_kernel(
         load_gamma(0, 0, 1)
         load_gamma(1, 0, 1)
         load_gamma(0, 1, 0)
-        load_w_scales()
+        load_w_scales(0)
         load_w(0)
         load_gamma(1, 1, 0)
+        load_w(1)
         load_gamma(0, 1, 1)
         load_gamma(1, 1, 1)
-        load_w(1)
+        load_w_scales(1)
+        load_w(2)
+        load_w(3)
         for g in range(F_PASSES):
             load_shapes(g)
 
+        turn_rot(7)
         turn_pair(0, 0, 0)
         turn_pair(1, 0, 1)
         strain_a_pair(0, 0)
@@ -324,36 +335,37 @@ def tile_laminate_shear_resultants_s9_kernel(
         strain_b(0, 1, (6, 7), range(4))
         turn(0, 1, 0, (1, 2))
         strain_a(1, 0, (1, 2), (0, 1))
-        order_w_scales()
-        ws(0, 1, "act", 256, 512)
-        ws(0, 1, "dve", 0, 256)
+        order_w_scales(0)
+        ws(0, 1, "act", 320, 512)
+        ws(0, 1, "dve", 0, 320)
         order_w(0)
         qs(0, 1)
+        order_w(1)
         strain_a(1, 0, (1, 2), (2, 3))
         turn(1, 1, 0, (3, 0))
         group(0, 0, (4, 5, 1, 2))
-        strain_b(1, 0, (3, 0), (3, 0, 1, 2))
+        strain_b(1, 0, (3, 0), (1, 0, 3, 2))
         turn(0, 1, 1, (4, 5))
         turn(1, 1, 1, (6, 7))
         strain_a(1, 1, (4, 5))
-        order_w(1)
+        order_w_scales(1)
         ws(1, 0)
-        group(0, 1, (1, 2, 3, 0), (1, 0, 3, 2))
+        order_w(2)
+        group(0, 1, (1, 2, 3, 0))
         strain_b(1, 1, (6, 7), (0, 1))
         qs(1, 0)
         strain_b(1, 1, (6, 7), (2, 3))
-        group(0, 2, (4, 5, 2, 1), (1, 0, 3, 2))
+        order_w(3)
+        group(0, 2, (4, 5, 1, 2), (1, 0, 3, 2))
         wf(0, 0)
         ws(1, 1)
         qf(0, 0)
-        group(0, 3, (0, 3, 6, 7), (1, 0, 3, 2))
+        group(0, 3, (3, 0, 6, 7), (1, 0, 3, 2))
         qs(1, 1)
         RA = (4, 5, 1, 2)
         RB = (3, 0, 6, 7)
-        group(1, 0, (5, 4, 1, 2), (1, 0, 3, 2))
-        group(1, 1, (3, 0, 7, 6), (1, 0, 3, 2))
-        group(1, 2, (4, 5, 2, 1), (3, 0, 1, 2))
-        group(1, 3, (6, 3, 0, 7), (1, 0, 3, 2))
+        for g in range(4):
+            group(1, g, (RA, RB)[g % 2], (1, 0, 3, 2))
         ww(0)
         wf(0, 1)
         qw(0)
@@ -372,26 +384,27 @@ def tile_laminate_shear_resultants_s9_kernel(
         qw(3)
         qf(0, 3)
         res4(0, 3, RA)
-        wf(1, 3, "act", 0, 256)
         wf(1, 2, "act", 0, 256)
-        wf(1, 3, "act", 256, 512)
+        wf(1, 3, "act", 0, 256)
         wf(1, 0, "dve", 0, 256)
         wf(1, 1, "dve", 0, 256)
-        for g in (0, 3, 2, 1):
+        for g in (0, 2, 3, 1):
             qf(1, g, 0, 256)
             res4(1, g, RB, (0, 1), 0, 1)
         for a in range(4):
             store(0, a, RA[a], "act")
+        wf(1, 3, "act", 256, 512)
         wf(1, 0, "dve", 256, 512)
         wf(1, 1, "dve", 256, 512)
-        for g in (3, 0, 1):
+        for g in (0, 1):
             qf(1, g, 256, 512)
-            res4(1, g, RB, (2, 3), 3, 2)
+            res4(1, g, RB, (2, 3), 0, 2)
         wf(1, 2, "dve", 256, 512)
         store(1, 0, RB[0], "act")
         store(1, 1, RB[1], "act")
-        qf(1, 2, 256, 512)
-        res4(1, 2, RB, (2, 3), 3, 2)
+        for g in (3, 2):
+            qf(1, g, 256, 512)
+            res4(1, g, RB, (2, 3), 0, 2)
         for lo in (0, 256):
             store(1, 2, RB[2], "act", lo, lo + 256)
             store(1, 3, RB[3], "dve", lo, lo + 256)

@@ -144,11 +144,10 @@ def tile_laminate_shear_resultants_s9_kernel(
                 prod["pair", ap, t] = d
 
         def strain_b_pair(ap, b):
-            if (0, 0) not in s_rows:
-                s_rows[0, 0] = sb("s_rows00", [P, PACK, HALF], BF16)
+            s_rows["pair", ap] = sb("s_first%d" % ap, [P, PACK, 256], BF16)
             for t in range(PACK):
                 nc.vector.scalar_tensor_tensor(
-                    out=s_rows[0, 0][:, t, ap * 256 : (ap + 1) * 256], in0=turned_pair(b, t), scalar=rot[:, t // 2, 2, t % 2 : t % 2 + 1],
+                    out=s_rows["pair", ap][:, t, :], in0=turned_pair(b, t), scalar=rot[:, t // 2, 2, t % 2 : t % 2 + 1],
                     in1=prod["pair", ap, t][:], op0=ALU.mult, op1=ALU.add,
                 )
 
@@ -173,12 +172,17 @@ def tile_laminate_shear_resultants_s9_kernel(
 
         woven = {}
 
-        def weave(key, rows, eng, lo=0, hi=512):
+        def weave(key, rows, eng, lo=0, hi=512, off=0):
             if key not in woven:
                 woven[key] = sb("woven_%s" % key, [P, 512, PACK], BF16, tag="woven", bufs=5)
             dst = woven[key][:, lo:hi, :].rearrange("p (c i) t -> p c t i", i=4)
-            src = rows[:, :, lo:hi].rearrange("p t (c i) -> p c t i", i=4)
-            if eng == "act":
+            src = rows[:, :, lo - off : hi - off].rearrange("p t (c i) -> p c t i", i=4)
+            if eng == "pool":
+                nc.gpsimd.tensor_scalar(
+                    out=woven[key][:, lo:hi, :], in0=rows[:, :, lo - off : hi - off].rearrange("p t c -> p c t"),
+                    scalar1=1.0, scalar2=0.0, op0=ALU.mult, op1=ALU.add,
+                )
+            elif eng == "act":
                 nc.scalar.copy(out=dst, in_=src)
             else:
                 nc.vector.tensor_copy(out=dst, in_=src)
@@ -284,8 +288,8 @@ def tile_laminate_shear_resultants_s9_kernel(
         def qs(h, kg):
             quantise("s%d%d" % (h, kg), E4M3)
 
-        def ww(g, eng="dve"):
-            weave("w%d" % g, shapes_raw[g], eng)
+        def ww(g, eng="dve", lo=0, hi=512):
+            weave("w%d" % g, shapes_raw[g], eng, lo, hi)
 
         def qw(g):
             quantise("w%d" % g, E4M3)
@@ -306,13 +310,14 @@ def tile_laminate_shear_resultants_s9_kernel(
         load_w_scales(0)
         load_w(0)
         load_gamma(1, 1, 0)
-        load_w(1)
         load_gamma(0, 1, 1)
+        load_w(1)
         load_gamma(1, 1, 1)
         load_w_scales(1)
         load_w(2)
+        load_shapes(0)
         load_w(3)
-        for g in range(F_PASSES):
+        for g in range(1, F_PASSES):
             load_shapes(g)
 
         turn_rot(7)
@@ -322,13 +327,13 @@ def tile_laminate_shear_resultants_s9_kernel(
         turn_pair(0, 1, 2)
         turn_pair(1, 1, 3)
         strain_b_pair(0, 1)
+        weave("s00", s_rows["pair", 0], "pool", 0, 256)
         strain_a_pair(1, 2)
         strain_b_pair(1, 3)
         turn_vectors(0)
         turn(0, 0, 1, (4, 5))
         turn(1, 0, 1, (6, 7))
-        ws(0, 0, "act", 384, 512)
-        ws(0, 0, "dve", 0, 384)
+        weave("s00", s_rows["pair", 1], "dve", 256, 512, 256)
         strain_a(0, 1, (4, 5))
         make_bias()
         qs(0, 0)
@@ -340,53 +345,57 @@ def tile_laminate_shear_resultants_s9_kernel(
         ws(0, 1, "dve", 0, 320)
         order_w(0)
         qs(0, 1)
-        order_w(1)
         strain_a(1, 0, (1, 2), (2, 3))
-        turn(1, 1, 0, (3, 0))
+        turn(1, 1, 0, (6, 7))
+        turn(0, 1, 1, (3, 0))
+        strain_a(1, 1, (3, 0), (0, 1))
         group(0, 0, (4, 5, 1, 2))
-        strain_b(1, 0, (3, 0), (1, 0, 3, 2))
-        turn(0, 1, 1, (4, 5))
+        strain_b(1, 0, (6, 7), (0, 1))
+        order_w(1)
+        strain_b(1, 0, (6, 7), (2, 3))
+        strain_a(1, 1, (3, 0), (2, 3))
         turn(1, 1, 1, (6, 7))
-        strain_a(1, 1, (4, 5))
+        group(0, 1, (3, 4, 5, 1))
         order_w_scales(1)
         ws(1, 0)
         order_w(2)
-        group(0, 1, (1, 2, 3, 0))
-        strain_b(1, 1, (6, 7), (0, 1))
         qs(1, 0)
-        strain_b(1, 1, (6, 7), (2, 3))
+        woven["w0"] = woven["s10"]
+        ww(0, "pool", 0, 352)
+        group(0, 2, (2, 0, 3, 4))
+        strain_b(1, 1, (6, 7), range(4))
         order_w(3)
-        group(0, 2, (4, 5, 1, 2), (1, 0, 3, 2))
-        wf(0, 0)
+        ww(0, "dve", 352, 512)
         ws(1, 1)
-        qf(0, 0)
-        group(0, 3, (3, 0, 6, 7), (1, 0, 3, 2))
+        qw(0)
         qs(1, 1)
-        RA = (4, 5, 1, 2)
-        RB = (3, 0, 6, 7)
+        group(0, 3, (5, 1, 6, 7), (1, 0, 3, 2))
+        RA = (0, 2, 4, 3)
+        RB = (1, 5, 7, 6)
         for g in range(4):
             group(1, g, (RA, RB)[g % 2], (1, 0, 3, 2))
-        ww(0)
-        wf(0, 1)
-        qw(0)
-        qf(0, 1)
+        wf(0, 0)
         ww(1)
-        wf(0, 2)
+        qf(0, 0)
         qw(1)
-        qf(0, 2)
+        wf(0, 1)
         ww(2)
+        qf(0, 1)
+        qw(2)
+        wf(0, 2)
+        ww(3)
+        qf(0, 2)
+        qw(3)
         res4(0, 0, RA)
         res4(0, 1, RA)
-        ww(3)
-        qw(2)
         res4(0, 2, RA)
-        wf(0, 3)
-        qw(3)
+        wf(0, 3, "act", 384, 512)
+        wf(0, 3, "dve", 0, 384)
+        wf(1, 0, "dve", 0, 256)
         qf(0, 3)
         res4(0, 3, RA)
         wf(1, 2, "act", 0, 256)
         wf(1, 3, "act", 0, 256)
-        wf(1, 0, "dve", 0, 256)
         wf(1, 1, "dve", 0, 256)
         for g in (0, 2, 3, 1):
             qf(1, g, 0, 256)

from contextlib import ExitStack

import concourse.mybir as mybir
from concourse.masks import make_identity

M, K, F, N = 1024, 1024, 2048, 512
FLOPS = 2 * M * K * F + 2 * M * F * N

F32 = mybir.dt.float32
BF16 = mybir.dt.bfloat16
I32 = mybir.dt.int32
U32 = mybir.dt.uint32
U8 = mybir.dt.uint8
E4M3 = mybir.dt.float8_e4m3fn_x4
E5M2 = mybir.dt.float8_e5m2_x4
E2M1 = mybir.dt.float4_e2m1fn_x4
ALU = mybir.AluOpType
ACT = mybir.ActivationFunctionType

P = 128
PACK = 4
PASS = P * PACK
HALF = 512
HALVES = M // HALF
K_PASSES = K // PASS
F_PASSES = F // PASS
RUN = 8


def tile_laminate_shear_resultants_s9_kernel(
    tc, gamma_xz, gamma_yz, cos_ply, sin_ply, stiff_words, stiff_scales, tau0, thick, shapes, out
):
    nc = tc.nc
    with ExitStack() as ctx:
        keep = ctx.enter_context(tc.tile_pool(name="keep", bufs=1))
        psum = ctx.enter_context(tc.psum_pool(name="psum", bufs=1))
        ctx.enter_context(tc.manual_schedule())

        def sb(name, shape, dtype, tag=None, bufs=1):
            return keep.tile(shape, dtype, name=name, tag=tag or name, bufs=bufs, align_bytes=64)

        bank = [psum.tile([P, 512], F32, name="bank%d" % b) for b in range(8)]

        rot_rows = sb("rot_rows", [P, PASS], BF16)
        nc.gpsimd.memset(rot_rows[:].bitcast(I32), 0)
        ident = sb("ident", [P, P], F32)
        ident_bf = sb("ident_bf", [P, P], BF16)
        make_identity(nc, ident[:])
        make_identity(nc, ident_bf[:])

        vec_raw = sb("vec_raw", [P, PASS], BF16)
        vec_rows = sb("vec_rows", [P, PASS], BF16)
        w_scale_raw = sb("w_scale_raw", [P, 2, K_PASSES, F // 2], U8)
        nc.vector.memset(vec_rows[:], 0.0)
        nc.vector.memset(w_scale_raw[:].rearrange("p c g n -> p (c g n)").bitcast(I32), 0)

        gamma = {}

        def load_gamma(x, h, kg):
            src = (gamma_xz, gamma_yz)[x]
            t = sb("gamma%d%d%d" % (x, h, kg), [P, 4, PASS], BF16)
            rows = src[h * HALF : (h + 1) * HALF, kg * PASS : (kg + 1) * PASS]
            nc.sync.dma_start(out=t[:], in_=rows.rearrange("(a p) k -> p a k", p=P))
            gamma[x, h, kg] = t

        warm = sb("warm", [P, 2], F32)

        rot = sb("rot", [P, 2, 4, 2], F32)

        def turn_rot(b):
            words = rot_rows[:].bitcast(F32)
            for u in range(2):
                nc.tensor.transpose(bank[b][:, u * P : (u + 1) * P], words[:, u::2], ident[:])
            view = bank[b][:].bitcast(BF16)[:, 0:PASS].rearrange("p (u r e) -> p u r e", u=2, e=2)
            nc.vector.tensor_copy(out=rot[:], in_=view[:, :, 0:4, :])

        def load_rot():
            for r, src in enumerate((cos_ply, sin_ply)):
                nc.sync.dma_start(out=rot_rows[2 * r : 2 * r + 2, :], in_=src.rearrange("(g c) -> g c", c=PASS))

        def load_vectors():
            for r, src in enumerate((tau0, thick)):
                nc.scalar.dma_start(out=vec_raw[4 * r : 4 * r + 4, :], in_=src.rearrange("(g c) -> g c", c=PASS))
            nc.scalar.activation(out=warm[:, 0:1], in_=ident[:, 0:1], func=ACT.Copy)
            nc.vector.tensor_copy(
                out=vec_rows[0:8, :].rearrange("r (t j i) -> r t j i", t=PACK, i=RUN),
                in_=vec_raw[0:8, :].rearrange("r (j t i) -> r t j i", t=PACK, i=RUN),
            )

        def load_w_scales(c):
            for q in range(4):
                nc.sync.dma_start(
                    out=w_scale_raw[32 * q : 32 * q + 4, c, :, :].bitcast(I32),
                    in_=stiff_scales[:, 4 * q : 4 * q + 4, c * 1024 : (c + 1) * 1024].rearrange("g r n -> r g n").bitcast(I32),
                )

        w_raw = {}

        def load_w(c):
            t = sb("w_raw%d" % c, [P, K_PASSES, 1024], U8)
            src = stiff_words[:, :, c * 1024 : (c + 1) * 1024].rearrange("g p n -> p g n")
            nc.sync.dma_start(out=t[:].bitcast(I32), in_=src.bitcast(I32))
            w_raw[c] = t

        shapes_raw = {}

        def load_shapes(g):
            t = sb("shapes_raw%d" % g, [P, PACK, N], BF16)
            src = shapes[g * PASS : (g + 1) * PASS, :].rearrange("(j t i) n -> t j i n", t=PACK, i=RUN)
            for s in range(PACK):
                nc.sync.dma_start(out=t[:, s, :], in_=src[s])
            shapes_raw[g] = t

        def turn(x, h, kg, banks):
            words = gamma[x, h, kg][:].bitcast(F32)
            for u in range(2):
                for a in range(4):
                    nc.tensor.transpose(bank[banks[u]][:, a * P : (a + 1) * P], words[:, a, u::2], ident[:])

        def turned(b, e):
            return bank[b][:].bitcast(BF16).rearrange("p (m e) -> p m e", e=2)[:, :, e]

        def load_pair(x, ap):
            src = (gamma_xz, gamma_yz)[x]
            t = sb("gamma_first%d%d" % (x, ap), [P, 2, PASS], BF16)
            rows = src[ap * 256 : (ap + 1) * 256, 0:PASS]
            nc.sync.dma_start(out=t[:], in_=rows.rearrange("(a p) k -> p a k", p=P))
            gamma[x, "pair", ap] = t

        def turn_pair(x, ap, b):
            words = gamma[x, "pair", ap][:].bitcast(F32)
            for u in range(2):
                for a in range(2):
                    c0 = (2 * u + a) * P
                    nc.tensor.transpose(bank[b][:, c0 : c0 + P], words[:, a, u::2], ident[:])

        def turned_pair(b, t):
            return bank[b][:].bitcast(BF16).rearrange("p (u m e) -> p u m e", u=2, e=2)[:, t // 2, :, t % 2]

        def strain_a_pair(ap, b):
            for t in range(PACK):
                d = sb("prod_first%d%d" % (ap, t), [P, 256], F32)
                nc.scalar.activation(out=d[:], in_=turned_pair(b, t), func=ACT.Copy, scale=rot[:, t // 2, 0, t % 2 : t % 2 + 1])
                prod["pair", ap, t] = d

        def strain_b_pair(ap, b):
            s_rows["pair", ap] = sb("s_first%d" % ap, [P, PACK, 256], BF16)
            for t in range(PACK):
                nc.vector.scalar_tensor_tensor(
                    out=s_rows["pair", ap][:, t, :], in0=turned_pair(b, t), scalar=rot[:, t // 2, 2, t % 2 : t % 2 + 1],
                    in1=prod["pair", ap, t][:], op0=ALU.mult, op1=ALU.add,
                )

        prod = {}

        def strain_a(h, kg, banks, ts=range(PACK)):
            for t in ts:
                d = sb("prod%d%d%d" % (h, kg, t), [P, HALF], F32, tag="prod", bufs=12)
                nc.scalar.activation(out=d[:], in_=turned(banks[t // 2], t % 2), func=ACT.Copy, scale=rot[:, t // 2, kg, t % 2 : t % 2 + 1])
                prod[h, kg, t] = d

        s_rows = {}

        def strain_b(h, kg, banks, ts):
            if (h, kg) not in s_rows:
                s_rows[h, kg] = sb("s_rows%d%d" % (h, kg), [P, PACK, HALF], BF16)
            for t in ts:
                nc.vector.scalar_tensor_tensor(
                    out=s_rows[h, kg][:, t, :], in0=turned(banks[t // 2], t % 2), scalar=rot[:, t // 2, 2 + kg, t % 2 : t % 2 + 1],
                    in1=prod[h, kg, t][:], op0=ALU.mult, op1=ALU.add,
                )

        woven = {}

        def weave(key, rows, eng, lo=0, hi=512, off=0):
            if key not in woven:
                woven[key] = sb("woven_%s" % key, [P, 512, PACK], BF16, tag="woven", bufs=5)
            dst = woven[key][:, lo:hi, :].rearrange("p (c i) t -> p c t i", i=4)
            src = rows[:, :, lo - off : hi - off].rearrange("p t (c i) -> p c t i", i=4)
            if eng == "pool":
                nc.gpsimd.tensor_scalar(
                    out=woven[key][:, lo:hi, :], in0=rows[:, :, lo - off : hi - off].rearrange("p t c -> p c t"),
                    scalar1=1.0, scalar2=0.0, op0=ALU.mult, op1=ALU.add,
                )
            elif eng == "act":
                nc.scalar.copy(out=dst, in_=src)
            else:
                nc.vector.tensor_copy(out=dst, in_=src)

        codes = {}

        def quantise(key, fmt, lo=0, hi=512):
            if key not in codes:
                codes[key] = (sb("codes_%s" % key, [P, 512], U32), sb("scales_%s" % key, [P, 512], U8))
            c, s = codes[key]
            nc.vector.quantize_mx(
                out=c[:, lo:hi].bitcast(fmt), scales=s[:, lo:hi], in_=woven[key][:, lo:hi, :].rearrange("p n t -> p (n t)")
            )

        vec = sb("vec", [P, PACK, 8], F32)
        bias = sb("bias", [P, PACK, F_PASSES], F32)

        def turn_vectors(b):
            view = bank[b][:].bitcast(BF16)[:, 0:PASS].rearrange("p (t r) -> p t r", r=P)
            for t in range(PACK):
                nc.tensor.transpose(view[:, t, :], vec_rows[:, t * P : (t + 1) * P], ident_bf[:])
            nc.scalar.copy(out=vec[:], in_=view[:, :, 0:8])

        def make_bias():
            nc.vector.tensor_tensor(out=bias[:], in0=vec[:, :, 0:4], in1=vec[:, :, 4:8], op=ALU.mult)

        w_codes = {}
        w_scale = sb("w_scale", [P, 2, PACK, K_PASSES * 2 * P], U8)

        def order_w(c):
            d = sb("w_codes%d" % c, [P, PACK, 512], U8)
            nc.vector.tensor_copy(
                out=d[:].bitcast(I32).rearrange("p t (b w) -> p b t w", w=4),
                in_=w_raw[c][:].rearrange("p g n -> p (g n)").bitcast(I32).rearrange("p (b t w) -> p b t w", t=PACK, w=4),
            )
            w_codes[c] = d

        def order_w_scales(c):
            nc.vector.tensor_copy(
                out=w_scale[:, c, :, :].bitcast(I32).rearrange("p t (b w) -> p t b w", w=2),
                in_=w_scale_raw[:, c, :, :].rearrange("p g n -> p (g n)").bitcast(I32).rearrange("p (b t w) -> p t b w", t=PACK, w=2),
            )

        def stress(h, g, t, b):
            for kg in range(K_PASSES):
                col = kg * 256
                scol = (2 * kg + g % 2) * P
                c, s = codes["s%d%d" % (h, kg)]
                nc.tensor.matmul_mx(
                    out=bank[b][:], lhsT=w_codes[g][:, t, col : col + 256].bitcast(E2M1),
                    lhsT_scale=w_scale[:, g // 2, t, scol : scol + P], rhs=c[:].bitcast(E4M3), rhs_scale=s[:],
                    start=(kg == 0), stop=(kg == K_PASSES - 1),
                )

        f_rows = {}

        def force(h, g, t, b, eng):
            if (h, g) not in f_rows:
                f_rows[h, g] = sb("f_rows%d%d" % (h, g), [P, PACK, HALF], BF16, tag="f_rows", bufs=8)
            if eng == "act":
                nc.scalar.activation(
                    out=f_rows[h, g][:, t, :], in_=bank[b][:], func=ACT.Identity,
                    scale=vec[:, t, 4 + g : 5 + g], bias=bias[:, t, g : g + 1],
                )
            else:
                nc.vector.tensor_scalar(
                    out=f_rows[h, g][:, t, :], in0=bank[b][:], scalar1=vec[:, t, g : g + 1],
                    scalar2=vec[:, t, 4 + g : 5 + g], op0=ALU.add, op1=ALU.mult,
                )

        def resultants(h, g, a, b, start, stop):
            c, s = codes["f%d%d" % (h, g)]
            wc, ws = codes["w%d" % g]
            nc.tensor.matmul_mx(
                out=bank[b][:], lhsT=c[:, a * P : (a + 1) * P].bitcast(E5M2), lhsT_scale=s[:, a * P : (a + 1) * P],
                rhs=wc[:].bitcast(E4M3), rhs_scale=ws[:], start=start, stop=stop,
            )

        def store(h, a, b, eng, lo=0, hi=N):
            d = sb("res%d%d_%d" % (h, a, lo), [P, hi - lo], F32)
            if eng == "act":
                nc.scalar.copy(out=d[:], in_=bank[b][:, lo:hi])
            else:
                nc.vector.tensor_copy(out=d[:], in_=bank[b][:, lo:hi])
            r0 = h * HALF + a * P
            nc.sync.dma_start(out=out[r0 : r0 + P, lo:hi], in_=d[:])

        def group(h, g, banks, order=(0, 1, 2, 3)):
            for t in range(PACK):
                stress(h, g, t, banks[t])
            for t in order:
                force(h, g, t, banks[t], "act")

        def wf(h, g, eng="dve", lo=0, hi=512):
            weave("f%d%d" % (h, g), f_rows[h, g], eng, lo, hi)

        def qf(h, g, lo=0, hi=512):
            quantise("f%d%d" % (h, g), E5M2, lo, hi)

        def ws(h, kg, eng="dve", lo=0, hi=512):
            weave("s%d%d" % (h, kg), s_rows[h, kg], eng, lo, hi)

        def qs(h, kg):
            quantise("s%d%d" % (h, kg), E4M3)

        def ww(g, eng="dve", lo=0, hi=512):
            weave("w%d" % g, shapes_raw[g], eng, lo, hi)

        def qw(g):
            quantise("w%d" % g, E4M3)

        def res4(h, g, banks, tiles=range(4), first=0, last=3):
            for a in tiles:
                resultants(h, g, a, banks[a], g == first, g == last)

        load_rot()
        load_pair(0, 0)
        load_pair(1, 0)
        load_vectors()
        load_pair(0, 1)
        load_pair(1, 1)
        load_gamma(0, 0, 1)
        load_gamma(1, 0, 1)
        load_gamma(0, 1, 0)
        load_w_scales(0)
        load_w(0)
        load_gamma(1, 1, 0)
        load_gamma(0, 1, 1)
        load_w(1)
        load_gamma(1, 1, 1)
        load_w_scales(1)
        load_w(2)
        load_shapes(0)
        load_w(3)
        for g in range(1, F_PASSES):
            load_shapes(g)

        turn_rot(7)
        turn_pair(0, 0, 0)
        turn_pair(1, 0, 1)
        strain_a_pair(0, 0)
        turn_pair(0, 1, 2)
        turn_pair(1, 1, 3)
        strain_b_pair(0, 1)
        weave("s00", s_rows["pair", 0], "pool", 0, 256)
        strain_a_pair(1, 2)
        strain_b_pair(1, 3)
        turn_vectors(0)
        turn(0, 0, 1, (4, 5))
        turn(1, 0, 1, (6, 7))
        weave("s00", s_rows["pair", 1], "dve", 256, 512, 256)
        strain_a(0, 1, (4, 5))
        make_bias()
        qs(0, 0)
        strain_b(0, 1, (6, 7), range(4))
        turn(0, 1, 0, (1, 2))
        strain_a(1, 0, (1, 2), (0, 1))
        order_w_scales(0)
        ws(0, 1, "act", 320, 512)
        ws(0, 1, "dve", 0, 320)
        order_w(0)
        qs(0, 1)
        strain_a(1, 0, (1, 2), (2, 3))
        turn(1, 1, 0, (6, 7))
        turn(0, 1, 1, (3, 0))
        strain_a(1, 1, (3, 0), (0, 1))
        group(0, 0, (4, 5, 1, 2))
        strain_b(1, 0, (6, 7), (0, 1))
        order_w(1)
        strain_b(1, 0, (6, 7), (2, 3))
        strain_a(1, 1, (3, 0), (2, 3))
        turn(1, 1, 1, (6, 7))
        group(0, 1, (3, 4, 5, 1))
        order_w_scales(1)
        ws(1, 0)
        order_w(2)
        qs(1, 0)
        woven["w0"] = woven["s10"]
        ww(0, "pool", 0, 352)
        group(0, 2, (2, 0, 3, 4))
        strain_b(1, 1, (6, 7), range(4))
        order_w(3)
        ww(0, "dve", 352, 512)
        ws(1, 1)
        qw(0)
        qs(1, 1)
        group(0, 3, (5, 1, 6, 7), (1, 0, 3, 2))
        RA = (0, 2, 4, 3)
        RB = (1, 5, 7, 6)
        for g in range(4):
            group(1, g, (RA, RB)[g % 2], (1, 0, 3, 2))
        wf(0, 0)
        ww(1)
        qf(0, 0)
        qw(1)
        wf(0, 1)
        ww(2)
        qf(0, 1)
        qw(2)
        wf(0, 2)
        ww(3)
        qf(0, 2)
        qw(3)
        res4(0, 0, RA)
        res4(0, 1, RA)
        res4(0, 2, RA)
        wf(0, 3, "act", 384, 512)
        wf(0, 3, "dve", 0, 384)
        wf(1, 0, "dve", 0, 256)
        qf(0, 3)
        res4(0, 3, RA)
        wf(1, 2, "act", 0, 256)
        wf(1, 3, "act", 0, 256)
        wf(1, 1, "dve", 0, 256)
        for g in (0, 2, 3, 1):
            qf(1, g, 0, 256)
            res4(1, g, RB, (0, 1), 0, 1)
        for a in range(4):
            store(0, a, RA[a], "act")
        wf(1, 3, "act", 256, 512)
        wf(1, 0, "dve", 256, 512)
        wf(1, 1, "dve", 256, 512)
        for g in (0, 1):
            qf(1, g, 256, 512)
            res4(1, g, RB, (2, 3), 0, 2)
        wf(1, 2, "dve", 256, 512)
        store(1, 0, RB[0], "act")
        store(1, 1, RB[1], "act")
        for g in (3, 2):
            qf(1, g, 256, 512)
            res4(1, g, RB, (2, 3), 0, 2)
        for lo in (0, 256):
            store(1, 2, RB[2], "act", lo, lo + 256)
            store(1, 3, RB[3], "dve", lo, lo + 256)
